import numpy as np, ml_dtypes
CORES = [76,84,92,100,108,116,124]
N = 7
import mx_ref
NC = 128
C2 = np.float32(0.28343)
BF = ml_dtypes.bfloat16
def cut(t, i, w=512):
    return t[:, w * i:w * i + w]
def tile(rs):
    return np.stack(rs, axis=2).reshape(128, -1).astype(BF)
def pick(b):
    s = np.zeros((128, 128, 4), np.float32)
    s[np.arange(128), np.arange(128), b] = 1.0
    return mx_ref.quantize(s.reshape(128, 512).astype(BF))
def setup_inputs(rng):
    def f(*shape):
        return mx_ref.flush((rng.standard_normal(shape, dtype=np.float32) * np.exp2(rng.integers(-2, 3, shape[:-1] + (1,)))).astype(BF))
    return {"b": f(N, 128, N * 512), "x": f(N, 128, 4 * NC)}
def setup_inputs_blocks(rng):
    d = setup_inputs(rng)
    for k in ("b", "x"): d[k] = mx_ref.spread(d[k], rng, 2)
    return d
def setup_inputs_wide(rng):
    d = setup_inputs(rng)
    for k in ("b", "x"): d[k] = mx_ref.flush((d[k].astype(np.float32) * np.exp2(rng.integers(-4, 5, (N, 1, 1))).astype(np.float32)).astype(BF))
    return d
def reference(b, x, own=None):
    S = [pick(t) for t in range(4)]
    h = np.zeros((N, 128, 512), BF)
    for c in range(N):
        for r in range(N):
            q = mx_ref.quantize(cut(b[r], c))
            P = [mx_ref.matmul(S[t], q) for t in range(4)]
            Z = P if r == 0 else [z + p for z, p in zip(Z, P)]
        h[c] = tile([np.maximum(Z[t], 0) * C2 for t in range(4)])
    use = h if own is None else own["h"]
    H = [mx_ref.quantize(use[j]) for j in range(N)]
    y = np.zeros((N, 128, N * NC), np.float32)
    for r in range(N):
        qx = mx_ref.quantize(x[r])
        for j in range(N):
            y[r][:, NC * j:NC * j + NC] = mx_ref.matmul(H[j], qx)
    return {"h": h, "y": y}

@@ -1,0 +1,271 @@
+import numpy as np
+from concourse.bass import DstId, RemoteDMATransfer
+from concourse.mybir import dt, AluOpType, ActivationFunctionType
+
+N = 7
+W = 128
+U8 = dt.uint8
+C2 = 0.28343
+CODES = "float8_e4m3fn_x4"
+
+SCRATCH = {
+    "bt": ("sbuf", [128, N * 512], "bfloat16"),
+    "xt": ("sbuf", [128, 512], "bfloat16"),
+    "one": ("sbuf", [128, 128], "bfloat16"),
+    "eye": ("sbuf", [128, 128], "bfloat16"),
+    "st": ("sbuf", [128, 2048], "bfloat16"),
+    "ht": ("sbuf", [128, 512], "bfloat16"),
+    "yt": ("sbuf", [128, N * 128], "float32"),
+    "bq": ("sbuf", [128, N * W], CODES), "bs": ("sbuf", [128, N * W], "uint8"),
+    "xq": ("sbuf", [128, W], CODES), "xs": ("sbuf", [128, W], "uint8"),
+    "sq": ("sbuf", [128, 4 * W], CODES), "ss": ("sbuf", [128, 4 * W], "uint8"),
+    "hq": ("sbuf", [128, W], CODES), "hs": ("sbuf", [128, W], "uint8"),
+    "gq": ("sbuf", [128, N * W], CODES), "gs": ("sbuf", [128, N * W], "uint8"),
+    "aq": ("sbuf", [128, N * W], CODES), "as": ("sbuf", [128, N * W], "uint8"),
+    "r1q": ("sbuf", [128, 4 * W], CODES), "r1s": ("sbuf", [128, 4 * W], "uint8"),
+    "r2q": ("sbuf", [128, W], CODES), "r2s": ("sbuf", [128, W], "uint8"),
+    "z": ("psum", [128, 2048], "float32"),
+    "yp": ("psum", [128, 2048], "float32"),
+}
+SEMAPHORES = (["one", "zero", "eye", "scp", "sq", "ldx", "qxx", "qa", "qb", "qd", "qo", "hr", "hq", "sth", "sty", "sta",
+               "r1", "r2", "loc1", "loc2"]
+              + ["ld%d" % i for i in range(N)] + ["z%d" % i for i in range(4)]
+              + ["p%d" % i for i in range(N)] + ["a%d" % i for i in range(N)]
+              + ["ym%d" % i for i in range(N)] + ["yc%d" % i for i in range(N)])
+
+
+def engines(m):
+    return [i for i in range(m.bit_length()) if (m >> i) & 1]
+
+
+def bits(es):
+    return sum(1 << e for e in es)
+
+
+def count(m):
+    return len(engines(m))
+
+
+def split(m, k):
+    e = engines(m)
+    q = len(e) // 4
+    if k == 1:
+        return [m]
+    if k == 2:
+        return [bits(e[:2 * q]), bits(e[2 * q:])]
+    if k == 3:
+        return [bits(e[:q]), bits(e[q:2 * q]), bits(e[2 * q:])]
+    return [bits(e[i * q:(i + 1) * q]) for i in range(4)]
+
+
+def split_back(m, k):
+    e = engines(m)
+    q = len(e) // 4
+    if k == 3:
+        return [bits(e[2 * q:3 * q]), bits(e[3 * q:]), bits(e[:2 * q])]
+    return split(m, k)
+
+
+def plan(T, topo, r):
+    me = T.cores[r]
+    others = [c for c in range(N) if c != r]
+    direct = [c for c in others if topo.may_write(me, T.cores[c])]
+    cross = [c for c in others if c not in direct]
+    direct = [c for c in direct if c > r] + [c for c in direct if c < r]
+    cross = [c for c in cross if c > r] + [c for c in cross if c < r]
+    ports = [k for k in range(128) if topo.chip(k) == topo.chip(me) and k != me
+             and all(topo.may_write(k, T.cores[c]) for c in cross)]
+    far = [k for k in ports if topo.die(k) != topo.die(me)]
+    near = [k for k in ports if topo.die(k) == topo.die(me)]
+    half = (len(cross) + 1) // 2
+    low = topo.mask(me, T.cores[direct[0]])
+    high = topo.mask(me, far[0]) & ~low
+    return {"me": me, "direct": direct, "cross": cross, "groups": [cross[:half], cross[half:]],
+            "codes": far[:2], "scales": near[0], "low": low, "high": high}
+
+
+def cols(i, n=1, w=W):
+    return slice(w * i, w * (i + n))
+
+
+def to(topo, dsts, mask, sem, src, dst):
+    ids = []
+    for c in dsts:
+        rid, pid, _ = topo.addr(c)
+        ids.append(DstId(rid=rid, pnc=pid))
+    return RemoteDMATransfer(dst_ids=ids, dma_engine_mask=mask, remote_sem=sem, srcs=[src], dsts=[dst] * len(ids))
+
+
+def out_mask(topo, k, dst):
+    return topo.mask(k, dst)
+
+
+def arrivals(T, topo, src, dst):
+    p = plan(T, topo, src)
+    if dst in p["direct"]:
+        i, k = p["direct"].index(dst), len(p["direct"])
+        return (count(split(p["low"], k)[i]) + count(split_back(p["low"], k)[i]), 2 * count(p["low"]))
+    n1 = n2 = 0
+    for k, grp in zip(p["codes"], p["groups"]):
+        if dst in grp:
+            m = topo.mask(k, T.cores[dst])
+            n1 += count(split(m, len(grp))[grp.index(dst)])
+            n2 += count(m)
+    m = topo.mask(p["scales"], T.cores[dst])
+    n1 += count(split(m, len(p["cross"]))[p["cross"].index(dst)])
+    n2 += count(m)
+    return n1, n2
+
+
+def relay_program(g, core, T, topo, r):
+    p = plan(T, topo, r)
+    if core in p["codes"]:
+        i = p["codes"].index(core)
+        grp = p["groups"][i]
+        bufs = [(T.r1q, T.gq), (T.r2q, T.aq)]
+    else:
+        grp = p["cross"]
+        bufs = [(T.r1s, T.gs), (T.r2s, T["as"])]
+    if not grp:
+        return
+
+    def view(t, i):
+        return t[:, cols(i)].bitcast(U8) if core in p["codes"] else t[:, cols(i)]
+
+    m = topo.mask(core, T.cores[grp[0]])
+    ms = split(m, len(grp))
+    here = count(p["high"])
+    g.wait_ge(T.sem.r1, here)
+    g.remote_dma_fused([to(topo, [T.cores[c]], ms[i], T.sem["p%d" % r], view(bufs[0][0], i), view(bufs[0][1], r))
+                        for i, c in enumerate(grp)], local_sem=T.sem.loc1)
+    g.wait_ge(T.sem.r2, here)
+    g.remote_dma_fused([to(topo, [T.cores[c] for c in grp], m, T.sem["a%d" % r], view(bufs[1][0], 0), view(bufs[1][1], r))],
+                       local_sem=T.sem.loc2)
+    g.wait_ge(T.sem.loc1, sum(count(x) for x in ms))
+    g.wait_ge(T.sem.loc2, count(m))
+
+
+def rank_program(g, core, T, topo):
+    r = T.rank_of(core)
+    if r is None:
+        for q in range(N):
+            if topo.chip(T.cores[q]) == topo.chip(core):
+                p = plan(T, topo, q)
+                if core in p["codes"] or core == p["scales"]:
+                    relay_program(g, core, T, topo, q)
+        return
+
+    p = plan(T, topo, r)
+    s = T.sem
+    direct, cross, groups = p["direct"], p["cross"], p["groups"]
+    nd, nc = len(direct), len(cross)
+    order = cross + direct + [r]
+    v, te, sc, sy = g.vector, g.tensor, g.scalar, g.sync
+
+    for i, c in enumerate(order):
+        (sy if i % 2 == 0 else sc).dma_start(T.bt[:, cols(i, 1, 512)], T.b[:, cols(c, 1, 512)]).then_inc(s["ld%d" % i], 16)
+    sc.dma_start(T.xt[:, :], T.x[:, :]).then_inc(s.ldx, 16)
+
+    v.memset(T.one[:], 1.0).then_inc(s.one, 1)
+    v.memset(T.st[:], 0.0).then_inc(s.zero, 1)
+    g.wait_ge(s.one, 1)
+    g.affine_select(T.eye[:], T.one[:], [[-1, 128]], AluOpType.is_equal, 0.0, 0, 1).then_inc(s.eye, 1)
+    v.wait_ge(s.eye, 1)
+    v.wait_ge(s.zero, 1)
+    for b in range(4):
+        v.tensor_copy(T.st[:, 512 * b + b:512 * b + 512:4], T.eye[:]).then_inc(s.scp, 1)
+
+    def quant(i, sem):
+        v.wait_ge(s["ld%d" % i], 16)
+        v.quantize_mx(T.bq[:, cols(i)], T.bs[:, cols(i)], T.bt[:, cols(i, 1, 512)]).then_inc(sem, 1)
+
+    n0, n1 = len(groups[0]), len(groups[1])
+    for i in range(nc):
+        quant(i, s.qa if i < n0 else s.qb)
+    for i in range(nc, nc + nd):
+        quant(i, s.qd)
+    v.wait_ge(s.scp, 4)
+    v.quantize_mx(T.sq[:], T.ss[:], T.st[:]).then_inc(s.sq, 1)
+    quant(N - 1, s.qo)
+    v.wait_ge(s.ldx, 16)
+    v.quantize_mx(T.xq[:], T.xs[:], T.xt[:]).then_inc(s.qxx, 1)
+
+    def hop(k, src, dst):
+        rid, pid, _ = topo.addr(k)
+        g.remote_dma(dst, src, s.r1, s.loc1, pid, rid, p["high"])
+
+    g.wait_ge(s.qa, n0)
+    hop(p["codes"][0], T.bq[:, cols(0, n0)].bitcast(U8), T.r1q[:, cols(0, n0)].bitcast(U8))
+    g.wait_ge(s.qb, n1)
+    hop(p["codes"][1], T.bq[:, cols(n0, n1)].bitcast(U8), T.r1q[:, cols(0, n1)].bitcast(U8))
+    hop(p["scales"], T.bs[:, cols(0, nc)], T.r1s[:, cols(0, nc)])
+    g.wait_ge(s.qd, nd)
+    mq, ms = split(p["low"], nd), split_back(p["low"], nd)
+    sem = s["p%d" % r]
+    g.remote_dma_fused([to(topo, [T.cores[c]], mq[i], sem, T.bq[:, cols(nc + i)].bitcast(U8), T.gq[:, cols(r)].bitcast(U8))
+                        for i, c in enumerate(direct)], local_sem=s.loc1)
+    g.remote_dma_fused([to(topo, [T.cores[c]], ms[i], sem, T.bs[:, cols(nc + i)], T.gs[:, cols(r)])
+                        for i, c in enumerate(direct)], local_sem=s.loc1)
+
+    te.wait_ge(s.sq, 1)
+    sources = [r] + [j for j in direct] + [j for j in cross]
+    for n, j in enumerate(sources):
+        if j == r:
+            te.wait_ge(s.qo, 1)
+            q, qs = T.bq[:, cols(N - 1)], T.bs[:, cols(N - 1)]
+        else:
+            te.wait_ge(s["p%d" % j], arrivals(T, topo, j, r)[0])
+            q, qs = T.gq[:, cols(j)], T.gs[:, cols(j)]
+        for b in range(4):
+            mm = te.matmul_mx(T.z[:, 512 * b:512 * b + 128], T.sq[:, cols(b)], T.ss[:, cols(b)], q, qs, n == 0, n == N - 1)
+            if n == N - 1:
+                mm.then_inc(s["z%d" % b], 1)
+
+    for b in range(4):
+        o, i = T.ht[:, b:512:4], T.z[:, 512 * b:512 * b + 128]
+        if b < 2:
+            sc.wait_ge(s["z%d" % b], 1)
+            sc.activation(o, i, ActivationFunctionType.Relu, scale=C2).then_inc(s.hr, 1)
+        else:
+            v.wait_ge(s["z%d" % b], 1)
+            v.tensor_scalar(o, i, 0.0, C2, AluOpType.max, AluOpType.mult).then_inc(s.hr, 1)
+    v.wait_ge(s.hr, 4)
+    v.quantize_mx(T.hq[:], T.hs[:], T.ht[:]).then_inc(s.hq, 1)
+
+    g.wait_ge(s.hq, 1)
+    sem = s["a%d" % r]
+    far = [T.cores[c] for c in direct]
+    g.remote_dma_fused([to(topo, p["codes"], p["high"], s.r2, T.hq[:].bitcast(U8), T.r2q[:].bitcast(U8)),
+                        to(topo, far, p["low"], sem, T.hq[:].bitcast(U8), T.aq[:, cols(r)].bitcast(U8))], local_sem=s.loc2)
+    g.remote_dma_fused([to(topo, [p["scales"]], p["high"], s.r2, T.hs[:], T.r2s[:]),
+                        to(topo, far, p["low"], sem, T.hs[:], T["as"][:, cols(r)])], local_sem=s.loc2)
+    loc2 = 2 * (count(p["high"]) + count(p["low"]))
+
+    banks = [T.yp[:, 512 * i:512 * i + 128] for i in range(4)] + [T.z[:, 512 * i:512 * i + 128] for i in range(4)]
+    te.wait_ge(s.qxx, 1)
+    for n, j in enumerate(sources):
+        if j == r:
+            te.wait_ge(s.hq, 1)
+            q, qs = T.hq[:], T.hs[:]
+        else:
+            te.wait_ge(s["a%d" % j], arrivals(T, topo, j, r)[1])
+            q, qs = T.aq[:, cols(j)], T["as"][:, cols(j)]
+        te.matmul_mx(banks[n], q, qs, T.xq[:], T.xs[:], True, True).then_inc(s["ym%d" % j], 1)
+    for n, j in enumerate(sources):
+        v.wait_ge(s["ym%d" % j], 1)
+        v.tensor_copy(T.yt[:, cols(j)], banks[n]).then_inc(s["yc%d" % j], 1)
+
+    sy.wait_ge(s.hr, 4)
+    sy.wait_ge(s.loc2, loc2)
+    sy.dma_start(T.h[:, :], T.ht[:]).then_inc(s.sth, 16)
+    ns = [0, 0]
+    for n, j in enumerate(sources):
+        k = n % 2
+        e = (sc, sy)[k]
+        e.wait_ge(s["yc%d" % j], 1)
+        e.dma_start(T.y[:, cols(j)], T.yt[:, cols(j)]).then_inc((s.sta, s.sty)[k], 16)
+        ns[k] += 16
+    sc.wait_ge(s.sta, ns[0])
+    sy.wait_ge(s.sty, ns[1])
+    sy.wait_ge(s.sth, 16)
+    g.wait_ge(s.loc1, 3 * count(p["high"]) + sum(count(x) for x in mq + ms))

@@ -13,12 +13,13 @@ SCRATCH = {
     "xt": ("sbuf", [128, 512], "bfloat16"),
     "one": ("sbuf", [128, 128], "bfloat16"),
     "eye": ("sbuf", [128, 128], "bfloat16"),
-    "st": ("sbuf", [128, 2048], "bfloat16"),
+    "st": ("sbuf", [128, 512], "bfloat16"),
     "ht": ("sbuf", [128, 512], "bfloat16"),
     "yt": ("sbuf", [128, N * 128], "float32"),
     "bq": ("sbuf", [128, N * W], CODES), "bs": ("sbuf", [128, N * W], "uint8"),
     "xq": ("sbuf", [128, W], CODES), "xs": ("sbuf", [128, W], "uint8"),
-    "sq": ("sbuf", [128, 4 * W], CODES), "ss": ("sbuf", [128, 4 * W], "uint8"),
+    "sq": ("sbuf", [128, W], CODES), "ss": ("sbuf", [128, W], "uint8"),
+    "tq": ("sbuf", [128, 3 * W], CODES), "ts": ("sbuf", [128, 3 * W], "uint8"),
     "hq": ("sbuf", [128, W], CODES), "hs": ("sbuf", [128, W], "uint8"),
     "gq": ("sbuf", [128, N * W], CODES), "gs": ("sbuf", [128, N * W], "uint8"),
     "aq": ("sbuf", [128, N * W], CODES), "as": ("sbuf", [128, N * W], "uint8"),
@@ -28,8 +29,8 @@ SCRATCH = {
     "yp": ("psum", [128, 2048], "float32"),
 }
 SEMAPHORES = (["one", "zero", "eye", "scp", "sq", "ldx", "qxx", "qa", "qb", "qd", "qo", "hr", "hq", "sth", "sty", "sta",
-               "r1", "r2", "loc1", "loc2"]
-              + ["ld%d" % i for i in range(N)] + ["z%d" % i for i in range(4)]
+               "r1", "r2", "loc0", "loc1", "loc2"]
+              + ["ld%d" % i for i in range(N)] + ["z%d" % i for i in range(4)] + ["s%d" % i for i in range(1, 4)]
               + ["p%d" % i for i in range(N)] + ["a%d" % i for i in range(N)]
               + ["ym%d" % i for i in range(N)] + ["yc%d" % i for i in range(N)])
 
@@ -81,7 +82,7 @@ def plan(T, topo, r):
     low = topo.mask(me, T.cores[direct[0]])
     high = topo.mask(me, far[0]) & ~low
     return {"me": me, "direct": direct, "cross": cross, "groups": [cross[:half], cross[half:]],
-            "codes": far[:2], "scales": near[0], "low": low, "high": high}
+            "codes": far[:2], "scales": near[0], "relays": far[:2] + near[:1], "low": low, "high": high}
 
 
 def cols(i, n=1, w=W):
@@ -94,10 +95,6 @@ def to(topo, dsts, mask, sem, src, dst):
         rid, pid, _ = topo.addr(c)
         ids.append(DstId(rid=rid, pnc=pid))
     return RemoteDMATransfer(dst_ids=ids, dma_engine_mask=mask, remote_sem=sem, srcs=[src], dsts=[dst] * len(ids))
-
-
-def out_mask(topo, k, dst):
-    return topo.mask(k, dst)
 
 
 def arrivals(T, topo, src, dst):
@@ -117,17 +114,28 @@ def arrivals(T, topo, src, dst):
     return n1, n2
 
 
+def make_s(g, T, b):
+    v, s = g.vector, T.sem
+    v.memset(T.one[:], 1.0).then_inc(s.one, 1)
+    v.memset(T.st[:], 0.0).then_inc(s.zero, 1)
+    g.wait_ge(s.one, 1)
+    g.affine_select(T.eye[:], T.one[:], [[-1, 128]], AluOpType.is_equal, 0.0, 0, 1).then_inc(s.eye, 1)
+    v.wait_ge(s.zero, 1)
+    v.wait_ge(s.eye, 1)
+    v.tensor_copy(T.st[:, b:512:4], T.eye[:]).then_inc(s.scp, 1)
+    v.wait_ge(s.scp, 1)
+    v.quantize_mx(T.sq[:], T.ss[:], T.st[:]).then_inc(s.sq, 1)
+
+
 def relay_program(g, core, T, topo, r):
     p = plan(T, topo, r)
+    s = T.sem
     if core in p["codes"]:
-        i = p["codes"].index(core)
-        grp = p["groups"][i]
+        grp = p["groups"][p["codes"].index(core)]
         bufs = [(T.r1q, T.gq), (T.r2q, T.aq)]
     else:
         grp = p["cross"]
         bufs = [(T.r1s, T.gs), (T.r2s, T["as"])]
-    if not grp:
-        return
 
     def view(t, i):
         return t[:, cols(i)].bitcast(U8) if core in p["codes"] else t[:, cols(i)]
@@ -135,24 +143,29 @@ def relay_program(g, core, T, topo, r):
     m = topo.mask(core, T.cores[grp[0]])
     ms = split(m, len(grp))
     here = count(p["high"])
-    g.wait_ge(T.sem.r1, here)
-    g.remote_dma_fused([to(topo, [T.cores[c]], ms[i], T.sem["p%d" % r], view(bufs[0][0], i), view(bufs[0][1], r))
-                        for i, c in enumerate(grp)], local_sem=T.sem.loc1)
-    g.wait_ge(T.sem.r2, here)
-    g.remote_dma_fused([to(topo, [T.cores[c] for c in grp], m, T.sem["a%d" % r], view(bufs[1][0], 0), view(bufs[1][1], r))],
-                       local_sem=T.sem.loc2)
-    g.wait_ge(T.sem.loc1, sum(count(x) for x in ms))
-    g.wait_ge(T.sem.loc2, count(m))
+    k = p["relays"].index(core)
+    make_s(g, T, k + 1)
+    rid, pid, _ = topo.addr(p["me"])
+    g.wait_ge(s.sq, 1)
+    g.remote_dma(T.tq[:, cols(k)].bitcast(U8), T.sq[:].bitcast(U8), s["s%d" % (k + 1)], s.loc0, pid, rid, m)
+    g.remote_dma(T.ts[:, cols(k)], T.ss[:], s["s%d" % (k + 1)], s.loc0, pid, rid, m)
+    g.wait_ge(s.r1, here)
+    g.remote_dma_fused([to(topo, [T.cores[c]], ms[i], s["p%d" % r], view(bufs[0][0], i), view(bufs[0][1], r))
+                        for i, c in enumerate(grp)], local_sem=s.loc1)
+    g.wait_ge(s.r2, here)
+    g.remote_dma_fused([to(topo, [T.cores[c] for c in grp], m, s["a%d" % r], view(bufs[1][0], 0), view(bufs[1][1], r))],
+                       local_sem=s.loc2)
+    g.wait_ge(s.loc0, 2 * count(m))
+    g.wait_ge(s.loc1, sum(count(x) for x in ms))
+    g.wait_ge(s.loc2, count(m))
 
 
 def rank_program(g, core, T, topo):
     r = T.rank_of(core)
     if r is None:
         for q in range(N):
-            if topo.chip(T.cores[q]) == topo.chip(core):
-                p = plan(T, topo, q)
-                if core in p["codes"] or core == p["scales"]:
-                    relay_program(g, core, T, topo, q)
+            if topo.chip(T.cores[q]) == topo.chip(core) and core in plan(T, topo, q)["relays"]:
+                relay_program(g, core, T, topo, q)
         return
 
     p = plan(T, topo, r)
@@ -166,14 +179,7 @@ def rank_program(g, core, T, topo):
         (sy if i % 2 == 0 else sc).dma_start(T.bt[:, cols(i, 1, 512)], T.b[:, cols(c, 1, 512)]).then_inc(s["ld%d" % i], 16)
     sc.dma_start(T.xt[:, :], T.x[:, :]).then_inc(s.ldx, 16)
 
-    v.memset(T.one[:], 1.0).then_inc(s.one, 1)
-    v.memset(T.st[:], 0.0).then_inc(s.zero, 1)
-    g.wait_ge(s.one, 1)
-    g.affine_select(T.eye[:], T.one[:], [[-1, 128]], AluOpType.is_equal, 0.0, 0, 1).then_inc(s.eye, 1)
-    v.wait_ge(s.eye, 1)
-    v.wait_ge(s.zero, 1)
-    for b in range(4):
-        v.tensor_copy(T.st[:, 512 * b + b:512 * b + 512:4], T.eye[:]).then_inc(s.scp, 1)
+    make_s(g, T, 0)
 
     def quant(i, sem):
         v.wait_ge(s["ld%d" % i], 16)
@@ -184,8 +190,6 @@ def rank_program(g, core, T, topo):
         quant(i, s.qa if i < n0 else s.qb)
     for i in range(nc, nc + nd):
         quant(i, s.qd)
-    v.wait_ge(s.scp, 4)
-    v.quantize_mx(T.sq[:], T.ss[:], T.st[:]).then_inc(s.sq, 1)
     quant(N - 1, s.qo)
     v.wait_ge(s.ldx, 16)
     v.quantize_mx(T.xq[:], T.xs[:], T.xt[:]).then_inc(s.qxx, 1)
@@ -207,7 +211,10 @@ def rank_program(g, core, T, topo):
     g.remote_dma_fused([to(topo, [T.cores[c]], ms[i], sem, T.bs[:, cols(nc + i)], T.gs[:, cols(r)])
                         for i, c in enumerate(direct)], local_sem=s.loc1)
 
+    S = [(T.sq[:], T.ss[:])] + [(T.tq[:, cols(k)], T.ts[:, cols(k)]) for k in range(3)]
     te.wait_ge(s.sq, 1)
+    for k, c in enumerate(p["relays"]):
+        te.wait_ge(s["s%d" % (k + 1)], 2 * count(topo.mask(c, T.cores[cross[0]])))
     sources = [r] + [j for j in direct] + [j for j in cross]
     for n, j in enumerate(sources):
         if j == r:
@@ -217,7 +224,7 @@ def rank_program(g, core, T, topo):
             te.wait_ge(s["p%d" % j], arrivals(T, topo, j, r)[0])
             q, qs = T.gq[:, cols(j)], T.gs[:, cols(j)]
         for b in range(4):
-            mm = te.matmul_mx(T.z[:, 512 * b:512 * b + 128], T.sq[:, cols(b)], T.ss[:, cols(b)], q, qs, n == 0, n == N - 1)
+            mm = te.matmul_mx(T.z[:, 512 * b:512 * b + 128], S[b][0], S[b][1], q, qs, n == 0, n == N - 1)
             if n == N - 1:
                 mm.then_inc(s["z%d" % b], 1)
 

@@ -23,14 +23,15 @@ SCRATCH = {
     "hq": ("sbuf", [128, W], CODES), "hs": ("sbuf", [128, W], "uint8"),
     "gq": ("sbuf", [128, N * W], CODES), "gs": ("sbuf", [128, N * W], "uint8"),
     "aq": ("sbuf", [128, N * W], CODES), "as": ("sbuf", [128, N * W], "uint8"),
-    "r1q": ("sbuf", [128, 4 * W], CODES), "r1s": ("sbuf", [128, 4 * W], "uint8"),
+    "r1q": ("sbuf", [128, 2 * W], CODES), "r1s": ("sbuf", [128, 2 * W], "uint8"),
     "r2q": ("sbuf", [128, W], CODES), "r2s": ("sbuf", [128, W], "uint8"),
     "z": ("psum", [128, 2048], "float32"),
     "yp": ("psum", [128, 2048], "float32"),
 }
-SEMAPHORES = (["one", "zero", "eye", "scp", "sq", "ldx", "qxx", "qa", "qb", "qd", "qo", "hr", "hq", "sth", "sty", "sta",
-               "r1", "r2", "loc0", "loc1", "loc2"]
-              + ["ld%d" % i for i in range(N)] + ["z%d" % i for i in range(4)] + ["s%d" % i for i in range(1, 4)]
+SEMAPHORES = (["one", "zero", "eye", "scp", "sq", "ldx", "qxx", "hr", "hq", "sth", "sty", "sta",
+               "r10", "r11", "r2", "loc0", "loc1", "loc2"]
+              + ["ld%d" % i for i in range(N)] + ["q%d" % i for i in range(N)]
+              + ["z%d" % i for i in range(4)] + ["s%d" % i for i in range(1, 4)]
               + ["p%d" % i for i in range(N)] + ["a%d" % i for i in range(N)]
               + ["ym%d" % i for i in range(N)] + ["yc%d" % i for i in range(N)])
 
@@ -39,32 +40,8 @@ def engines(m):
     return [i for i in range(m.bit_length()) if (m >> i) & 1]
 
 
-def bits(es):
-    return sum(1 << e for e in es)
-
-
 def count(m):
     return len(engines(m))
-
-
-def split(m, k):
-    e = engines(m)
-    q = len(e) // 4
-    if k == 1:
-        return [m]
-    if k == 2:
-        return [bits(e[:2 * q]), bits(e[2 * q:])]
-    if k == 3:
-        return [bits(e[:q]), bits(e[q:2 * q]), bits(e[2 * q:])]
-    return [bits(e[i * q:(i + 1) * q]) for i in range(4)]
-
-
-def split_back(m, k):
-    e = engines(m)
-    q = len(e) // 4
-    if k == 3:
-        return [bits(e[2 * q:3 * q]), bits(e[3 * q:]), bits(e[:2 * q])]
-    return split(m, k)
 
 
 def plan(T, topo, r):
@@ -76,13 +53,20 @@ def plan(T, topo, r):
     cross = [c for c in cross if c > r] + [c for c in cross if c < r]
     ports = [k for k in range(128) if topo.chip(k) == topo.chip(me) and k != me
              and all(topo.may_write(k, T.cores[c]) for c in cross)]
-    far = [k for k in ports if topo.die(k) != topo.die(me)]
-    near = [k for k in ports if topo.die(k) == topo.die(me)]
-    half = (len(cross) + 1) // 2
+    far = [k for k in ports if topo.die(k) != topo.die(me)][:2]
+    near = [k for k in ports if topo.die(k) == topo.die(me)][:2]
     low = topo.mask(me, T.cores[direct[0]])
     high = topo.mask(me, far[0]) & ~low
-    return {"me": me, "direct": direct, "cross": cross, "groups": [cross[:half], cross[half:]],
-            "codes": far[:2], "scales": near[0], "relays": far[:2] + near[:1], "low": low, "high": high}
+    n = len(cross)
+    share = [list(range(0, n, 2)), list(range(1, n, 2)), list(range(0, 2)), list(range(2, n))]
+    return {"me": me, "direct": direct, "cross": cross, "far": far, "near": near, "relays": far + near, "share": share,
+            "low": low, "high": high, "out": topo.mask(far[0], T.cores[cross[0]])}
+
+
+def due(T, topo, r):
+    p = plan(T, topo, r)
+    return (sorted(p["direct"], key=lambda j: plan(T, topo, j)["direct"].index(r))
+            + sorted(p["cross"], key=lambda j: plan(T, topo, j)["cross"].index(r)))
 
 
 def cols(i, n=1, w=W):
@@ -95,23 +79,6 @@ def to(topo, dsts, mask, sem, src, dst):
         rid, pid, _ = topo.addr(c)
         ids.append(DstId(rid=rid, pnc=pid))
     return RemoteDMATransfer(dst_ids=ids, dma_engine_mask=mask, remote_sem=sem, srcs=[src], dsts=[dst] * len(ids))
-
-
-def arrivals(T, topo, src, dst):
-    p = plan(T, topo, src)
-    if dst in p["direct"]:
-        i, k = p["direct"].index(dst), len(p["direct"])
-        return (count(split(p["low"], k)[i]) + count(split_back(p["low"], k)[i]), 2 * count(p["low"]))
-    n1 = n2 = 0
-    for k, grp in zip(p["codes"], p["groups"]):
-        if dst in grp:
-            m = topo.mask(k, T.cores[dst])
-            n1 += count(split(m, len(grp))[grp.index(dst)])
-            n2 += count(m)
-    m = topo.mask(p["scales"], T.cores[dst])
-    n1 += count(split(m, len(p["cross"]))[p["cross"].index(dst)])
-    n2 += count(m)
-    return n1, n2
 
 
 def make_s(g, T, b):
@@ -127,36 +94,42 @@ def make_s(g, T, b):
     v.quantize_mx(T.sq[:], T.ss[:], T.st[:]).then_inc(s.sq, 1)
 
 
+PARTS = [(1, 0, W), (2, 0, W), (3, 0, W // 2), (3, W // 2, W // 2)]
+
+
+def hop_mask(p, n):
+    return p["low"] if n == 1 else p["high"]
+
+
 def relay_program(g, core, T, topo, r):
     p = plan(T, topo, r)
     s = T.sem
-    if core in p["codes"]:
-        grp = p["groups"][p["codes"].index(core)]
-        bufs = [(T.r1q, T.gq), (T.r2q, T.aq)]
-    else:
-        grp = p["cross"]
-        bufs = [(T.r1s, T.gs), (T.r2s, T["as"])]
+    n = p["relays"].index(core)
+    dsts = [p["cross"][i] for i in p["share"][n]]
+    codes = core in p["far"]
+    m = p["out"]
 
     def view(t, i):
-        return t[:, cols(i)].bitcast(U8) if core in p["codes"] else t[:, cols(i)]
+        return t[:, cols(i)].bitcast(U8) if codes else t[:, cols(i)]
 
-    m = topo.mask(core, T.cores[grp[0]])
-    ms = split(m, len(grp))
-    here = count(p["high"])
-    k = p["relays"].index(core)
-    make_s(g, T, k + 1)
+    b, c0, nc = PARTS[n]
+    make_s(g, T, b)
     rid, pid, _ = topo.addr(p["me"])
+    d0 = W * (b - 1) + c0
     g.wait_ge(s.sq, 1)
-    g.remote_dma(T.tq[:, cols(k)].bitcast(U8), T.sq[:].bitcast(U8), s["s%d" % (k + 1)], s.loc0, pid, rid, m)
-    g.remote_dma(T.ts[:, cols(k)], T.ss[:], s["s%d" % (k + 1)], s.loc0, pid, rid, m)
-    g.wait_ge(s.r1, here)
-    g.remote_dma_fused([to(topo, [T.cores[c]], ms[i], s["p%d" % r], view(bufs[0][0], i), view(bufs[0][1], r))
-                        for i, c in enumerate(grp)], local_sem=s.loc1)
-    g.wait_ge(s.r2, here)
-    g.remote_dma_fused([to(topo, [T.cores[c] for c in grp], m, s["a%d" % r], view(bufs[1][0], 0), view(bufs[1][1], r))],
+    g.remote_dma(T.tq[:, d0:d0 + nc].bitcast(U8), T.sq[:, c0:c0 + nc].bitcast(U8), s["s%d" % b], s.loc0, pid, rid, m)
+    g.remote_dma(T.ts[:, d0:d0 + nc], T.ss[:, c0:c0 + nc], s["s%d" % b], s.loc0, pid, rid, m)
+    src, dst = (T.r1q, T.gq) if codes else (T.r1s, T.gs)
+    for i, c in enumerate(dsts):
+        if codes or i == 0:
+            g.wait_ge(s["r1%d" % i], count(hop_mask(p, n)))
+        g.remote_dma_fused([to(topo, [T.cores[c]], m, s["p%d" % r], view(src, i), view(dst, r))], local_sem=s.loc1)
+    src, dst = (T.r2q, T.aq) if codes else (T.r2s, T["as"])
+    g.wait_ge(s.r2, count(p["high"]))
+    g.remote_dma_fused([to(topo, [T.cores[c] for c in dsts], m, s["a%d" % r], view(src, 0), view(dst, r))],
                        local_sem=s.loc2)
     g.wait_ge(s.loc0, 2 * count(m))
-    g.wait_ge(s.loc1, sum(count(x) for x in ms))
+    g.wait_ge(s.loc1, len(dsts) * count(m))
     g.wait_ge(s.loc2, count(m))
 
 
@@ -170,7 +143,7 @@ def rank_program(g, core, T, topo):
 
     p = plan(T, topo, r)
     s = T.sem
-    direct, cross, groups = p["direct"], p["cross"], p["groups"]
+    direct, cross = p["direct"], p["cross"]
     nd, nc = len(direct), len(cross)
     order = cross + direct + [r]
     v, te, sc, sy = g.vector, g.tensor, g.scalar, g.sync
@@ -181,48 +154,50 @@ def rank_program(g, core, T, topo):
 
     make_s(g, T, 0)
 
-    def quant(i, sem):
+    for i in range(N):
         v.wait_ge(s["ld%d" % i], 16)
-        v.quantize_mx(T.bq[:, cols(i)], T.bs[:, cols(i)], T.bt[:, cols(i, 1, 512)]).then_inc(sem, 1)
-
-    n0, n1 = len(groups[0]), len(groups[1])
-    for i in range(nc):
-        quant(i, s.qa if i < n0 else s.qb)
-    for i in range(nc, nc + nd):
-        quant(i, s.qd)
-    quant(N - 1, s.qo)
+        v.quantize_mx(T.bq[:, cols(i)], T.bs[:, cols(i)], T.bt[:, cols(i, 1, 512)]).then_inc(s["q%d" % i], 1)
     v.wait_ge(s.ldx, 16)
     v.quantize_mx(T.xq[:], T.xs[:], T.xt[:]).then_inc(s.qxx, 1)
 
-    def hop(k, src, dst):
-        rid, pid, _ = topo.addr(k)
-        g.remote_dma(dst, src, s.r1, s.loc1, pid, rid, p["high"])
+    def hop(n, sem, dst, src):
+        rid, pid, _ = topo.addr(p["relays"][n])
+        g.remote_dma(dst, src, sem, s.loc1, pid, rid, hop_mask(p, n))
 
-    g.wait_ge(s.qa, n0)
-    hop(p["codes"][0], T.bq[:, cols(0, n0)].bitcast(U8), T.r1q[:, cols(0, n0)].bitcast(U8))
-    g.wait_ge(s.qb, n1)
-    hop(p["codes"][1], T.bq[:, cols(n0, n1)].bitcast(U8), T.r1q[:, cols(0, n1)].bitcast(U8))
-    hop(p["scales"], T.bs[:, cols(0, nc)], T.r1s[:, cols(0, nc)])
-    g.wait_ge(s.qd, nd)
-    mq, ms = split(p["low"], nd), split_back(p["low"], nd)
-    sem = s["p%d" % r]
-    g.remote_dma_fused([to(topo, [T.cores[c]], mq[i], sem, T.bq[:, cols(nc + i)].bitcast(U8), T.gq[:, cols(r)].bitcast(U8))
-                        for i, c in enumerate(direct)], local_sem=s.loc1)
-    g.remote_dma_fused([to(topo, [T.cores[c]], ms[i], sem, T.bs[:, cols(nc + i)], T.gs[:, cols(r)])
-                        for i, c in enumerate(direct)], local_sem=s.loc1)
+    loc1 = sum(count(hop_mask(p, i % 2)) for i in range(nc)) + 2 * count(p["high"])
+    for i in range(nc):
+        g.wait_ge(s["q%d" % i], 1)
+        n, k = i % 2, i // 2
+        hop(n, s["r1%d" % k], T.r1q[:, cols(k)].bitcast(U8), T.bq[:, cols(i)].bitcast(U8))
+        if i == 1:
+            hop(2, s.r10, T.r1s[:, cols(0, 2)], T.bs[:, cols(0, 2)])
+    hop(3, s.r10, T.r1s[:, cols(0, nc - 2)], T.bs[:, cols(2, nc - 2)])
+
+    def send(i, src, dst):
+        g.remote_dma_fused([to(topo, [T.cores[direct[i]]], p["low"], s["p%d" % r], src, dst)], local_sem=s.loc1)
+
+    for i in range(nd):
+        g.wait_ge(s["q%d" % (nc + i)], 1)
+        send(i, T.bq[:, cols(nc + i)].bitcast(U8), T.gq[:, cols(r)].bitcast(U8))
+        send(i, T.bs[:, cols(nc + i)], T.gs[:, cols(r)])
+    loc1 += 2 * nd * count(p["low"])
 
     S = [(T.sq[:], T.ss[:])] + [(T.tq[:, cols(k)], T.ts[:, cols(k)]) for k in range(3)]
     te.wait_ge(s.sq, 1)
-    for k, c in enumerate(p["relays"]):
-        te.wait_ge(s["s%d" % (k + 1)], 2 * count(topo.mask(c, T.cores[cross[0]])))
-    sources = [r] + [j for j in direct] + [j for j in cross]
-    for n, j in enumerate(sources):
+    for b in range(1, 4):
+        te.wait_ge(s["s%d" % b], sum(2 * count(p["out"]) for x in PARTS if x[0] == b))
+    sources = [r] + due(T, topo, r)
+
+    def arrived(sem, mine, j):
         if j == r:
-            te.wait_ge(s.qo, 1)
-            q, qs = T.bq[:, cols(N - 1)], T.bs[:, cols(N - 1)]
+            te.wait_ge(mine, 1)
         else:
-            te.wait_ge(s["p%d" % j], arrivals(T, topo, j, r)[0])
-            q, qs = T.gq[:, cols(j)], T.gs[:, cols(j)]
+            q = plan(T, topo, j)
+            te.wait_ge(s["%s%d" % (sem, j)], 2 * count(q["low"] if r in q["direct"] else q["out"]))
+
+    for n, j in enumerate(sources):
+        arrived("p", s["q%d" % (N - 1)], j)
+        q, qs = (T.bq[:, cols(N - 1)], T.bs[:, cols(N - 1)]) if j == r else (T.gq[:, cols(j)], T.gs[:, cols(j)])
         for b in range(4):
             mm = te.matmul_mx(T.z[:, 512 * b:512 * b + 128], S[b][0], S[b][1], q, qs, n == 0, n == N - 1)
             if n == N - 1:
@@ -230,7 +205,7 @@ def rank_program(g, core, T, topo):
 
     for b in range(4):
         o, i = T.ht[:, b:512:4], T.z[:, 512 * b:512 * b + 128]
-        if b < 2:
+        if b % 2 == 0:
             sc.wait_ge(s["z%d" % b], 1)
             sc.activation(o, i, ActivationFunctionType.Relu, scale=C2).then_inc(s.hr, 1)
         else:
@@ -241,38 +216,39 @@ def rank_program(g, core, T, topo):
 
     g.wait_ge(s.hq, 1)
     sem = s["a%d" % r]
-    far = [T.cores[c] for c in direct]
-    g.remote_dma_fused([to(topo, p["codes"], p["high"], s.r2, T.hq[:].bitcast(U8), T.r2q[:].bitcast(U8)),
-                        to(topo, far, p["low"], sem, T.hq[:].bitcast(U8), T.aq[:, cols(r)].bitcast(U8))], local_sem=s.loc2)
-    g.remote_dma_fused([to(topo, [p["scales"]], p["high"], s.r2, T.hs[:], T.r2s[:]),
-                        to(topo, far, p["low"], sem, T.hs[:], T["as"][:, cols(r)])], local_sem=s.loc2)
+    ranks = [T.cores[c] for c in direct]
+    for relays, src, mid, dst in ((p["far"], T.hq[:].bitcast(U8), T.r2q[:].bitcast(U8), T.aq[:, cols(r)].bitcast(U8)),
+                                  (p["near"], T.hs[:], T.r2s[:], T["as"][:, cols(r)])):
+        g.remote_dma_fused([to(topo, relays, p["high"], s.r2, src, mid), to(topo, ranks, p["low"], sem, src, dst)],
+                           local_sem=s.loc2)
     loc2 = 2 * (count(p["high"]) + count(p["low"]))
 
     banks = [T.yp[:, 512 * i:512 * i + 128] for i in range(4)] + [T.z[:, 512 * i:512 * i + 128] for i in range(4)]
     te.wait_ge(s.qxx, 1)
     for n, j in enumerate(sources):
-        if j == r:
-            te.wait_ge(s.hq, 1)
-            q, qs = T.hq[:], T.hs[:]
-        else:
-            te.wait_ge(s["a%d" % j], arrivals(T, topo, j, r)[1])
-            q, qs = T.aq[:, cols(j)], T["as"][:, cols(j)]
+        arrived("a", s.hq, j)
+        q, qs = (T.hq[:], T.hs[:]) if j == r else (T.aq[:, cols(j)], T["as"][:, cols(j)])
         te.matmul_mx(banks[n], q, qs, T.xq[:], T.xs[:], True, True).then_inc(s["ym%d" % j], 1)
-    for n, j in enumerate(sources):
-        v.wait_ge(s["ym%d" % j], 1)
-        v.tensor_copy(T.yt[:, cols(j)], banks[n]).then_inc(s["yc%d" % j], 1)
 
-    sy.wait_ge(s.hr, 4)
-    sy.wait_ge(s.loc2, loc2)
-    sy.dma_start(T.h[:, :], T.ht[:]).then_inc(s.sth, 16)
     ns = [0, 0]
     for n, j in enumerate(sources):
+        if n == 1:
+            sy.wait_ge(s.hr, 4)
+            sy.wait_ge(s["ym%d" % j], 1)
+            sy.dma_start(T.h[:, :], T.ht[:]).then_inc(s.sth, 16)
         k = n % 2
-        e = (sc, sy)[k]
+        if k == 0:
+            v.wait_ge(s["ym%d" % j], 1)
+            v.tensor_copy(T.yt[:, cols(j)], banks[n]).then_inc(s["yc%d" % j], 1)
+        else:
+            sc.wait_ge(s["ym%d" % j], 1)
+            sc.activation(T.yt[:, cols(j)], banks[n], ActivationFunctionType.Copy).then_inc(s["yc%d" % j], 1)
+        e = (sy, sc)[k]
         e.wait_ge(s["yc%d" % j], 1)
-        e.dma_start(T.y[:, cols(j)], T.yt[:, cols(j)]).then_inc((s.sta, s.sty)[k], 16)
+        e.dma_start(T.y[:, cols(j)], T.yt[:, cols(j)]).then_inc((s.sty, s.sta)[k], 16)
         ns[k] += 16
-    sc.wait_ge(s.sta, ns[0])
-    sy.wait_ge(s.sty, ns[1])
+    sc.wait_ge(s.sta, ns[1])
+    sy.wait_ge(s.sty, ns[0])
     sy.wait_ge(s.sth, 16)
-    g.wait_ge(s.loc1, 3 * count(p["high"]) + sum(count(x) for x in mq + ms))
+    g.wait_ge(s.loc1, loc1)
+    g.wait_ge(s.loc2, loc2)

import numpy as np
from concourse.bass import DstId, RemoteDMATransfer
from concourse.mybir import dt, AluOpType, ActivationFunctionType

N = 7
W = 128
U8 = dt.uint8
C2 = 0.28343
CODES = "float8_e4m3fn_x4"

SCRATCH = {
    "bt": ("sbuf", [128, N * 512], "bfloat16"),
    "xt": ("sbuf", [128, 512], "bfloat16"),
    "one": ("sbuf", [128, 128], "bfloat16"),
    "eye": ("sbuf", [128, 128], "bfloat16"),
    "st": ("sbuf", [128, 512], "bfloat16"),
    "ht": ("sbuf", [128, 512], "bfloat16"),
    "yt": ("sbuf", [128, N * 128], "float32"),
    "bq": ("sbuf", [128, N * W], CODES), "bs": ("sbuf", [128, N * W], "uint8"),
    "xq": ("sbuf", [128, W], CODES), "xs": ("sbuf", [128, W], "uint8"),
    "sq": ("sbuf", [128, W], CODES), "ss": ("sbuf", [128, W], "uint8"),
    "tq": ("sbuf", [128, 3 * W], CODES), "ts": ("sbuf", [128, 3 * W], "uint8"),
    "hq": ("sbuf", [128, W], CODES), "hs": ("sbuf", [128, W], "uint8"),
    "gq": ("sbuf", [128, N * W], CODES), "gs": ("sbuf", [128, N * W], "uint8"),
    "aq": ("sbuf", [128, N * W], CODES), "as": ("sbuf", [128, N * W], "uint8"),
    "r1q": ("sbuf", [128, 2 * W], CODES), "r1s": ("sbuf", [128, 2 * W], "uint8"),
    "r2q": ("sbuf", [128, W], CODES), "r2s": ("sbuf", [128, W], "uint8"),
    "z": ("psum", [128, 2048], "float32"),
    "yp": ("psum", [128, 2048], "float32"),
}
SEMAPHORES = (["one", "zero", "eye", "scp", "sq", "ldx", "qxx", "hr", "hq", "sth", "sty", "sta",
               "r10", "r11", "r2", "loc0", "loc1", "loc2"]
              + ["ld%d" % i for i in range(N)] + ["q%d" % i for i in range(N)]
              + ["z%d" % i for i in range(4)] + ["s%d" % i for i in range(1, 4)]
              + ["p%d" % i for i in range(N)] + ["a%d" % i for i in range(N)]
              + ["ym%d" % i for i in range(N)] + ["yc%d" % i for i in range(N)])


def engines(m):
    return [i for i in range(m.bit_length()) if (m >> i) & 1]


def count(m):
    return len(engines(m))


def plan(T, topo, r):
    me = T.cores[r]
    others = [c for c in range(N) if c != r]
    direct = [c for c in others if topo.may_write(me, T.cores[c])]
    cross = [c for c in others if c not in direct]
    direct = [c for c in direct if c > r] + [c for c in direct if c < r]
    cross = [c for c in cross if c > r] + [c for c in cross if c < r]
    ports = [k for k in range(128) if topo.chip(k) == topo.chip(me) and k != me
             and all(topo.may_write(k, T.cores[c]) for c in cross)]
    far = [k for k in ports if topo.die(k) != topo.die(me)][:2]
    near = [k for k in ports if topo.die(k) == topo.die(me)][:2]
    low = topo.mask(me, T.cores[direct[0]])
    high = topo.mask(me, far[0]) & ~low
    n = len(cross)
    share = [list(range(0, n, 2)), list(range(1, n, 2)), list(range(0, 2)), list(range(2, n))]
    return {"me": me, "direct": direct, "cross": cross, "far": far, "near": near, "relays": far + near, "share": share,
            "low": low, "high": high, "out": topo.mask(far[0], T.cores[cross[0]])}


def due(T, topo, r):
    p = plan(T, topo, r)
    return (sorted(p["direct"], key=lambda j: plan(T, topo, j)["direct"].index(r))
            + sorted(p["cross"], key=lambda j: plan(T, topo, j)["cross"].index(r)))


def cols(i, n=1, w=W):
    return slice(w * i, w * (i + n))


def to(topo, dsts, mask, sem, src, dst):
    ids = []
    for c in dsts:
        rid, pid, _ = topo.addr(c)
        ids.append(DstId(rid=rid, pnc=pid))
    return RemoteDMATransfer(dst_ids=ids, dma_engine_mask=mask, remote_sem=sem, srcs=[src], dsts=[dst] * len(ids))


def make_s(g, T, b):
    v, s = g.vector, T.sem
    v.memset(T.one[:], 1.0).then_inc(s.one, 1)
    v.memset(T.st[:], 0.0).then_inc(s.zero, 1)
    g.wait_ge(s.one, 1)
    g.affine_select(T.eye[:], T.one[:], [[-1, 128]], AluOpType.is_equal, 0.0, 0, 1).then_inc(s.eye, 1)
    v.wait_ge(s.zero, 1)
    v.wait_ge(s.eye, 1)
    v.tensor_copy(T.st[:, b:512:4], T.eye[:]).then_inc(s.scp, 1)
    v.wait_ge(s.scp, 1)
    v.quantize_mx(T.sq[:], T.ss[:], T.st[:]).then_inc(s.sq, 1)


PARTS = [(1, 0, W), (2, 0, W), (3, 0, W // 2), (3, W // 2, W // 2)]


def hop_mask(p, n):
    return p["low"] if n == 1 else p["high"]


def relay_program(g, core, T, topo, r):
    p = plan(T, topo, r)
    s = T.sem
    n = p["relays"].index(core)
    dsts = [p["cross"][i] for i in p["share"][n]]
    codes = core in p["far"]
    m = p["out"]

    def view(t, i):
        return t[:, cols(i)].bitcast(U8) if codes else t[:, cols(i)]

    b, c0, nc = PARTS[n]
    make_s(g, T, b)
    rid, pid, _ = topo.addr(p["me"])
    d0 = W * (b - 1) + c0
    g.wait_ge(s.sq, 1)
    g.remote_dma(T.tq[:, d0:d0 + nc].bitcast(U8), T.sq[:, c0:c0 + nc].bitcast(U8), s["s%d" % b], s.loc0, pid, rid, m)
    g.remote_dma(T.ts[:, d0:d0 + nc], T.ss[:, c0:c0 + nc], s["s%d" % b], s.loc0, pid, rid, m)
    src, dst = (T.r1q, T.gq) if codes else (T.r1s, T.gs)
    for i, c in enumerate(dsts):
        if codes or i == 0:
            g.wait_ge(s["r1%d" % i], count(hop_mask(p, n)))
        g.remote_dma_fused([to(topo, [T.cores[c]], m, s["p%d" % r], view(src, i), view(dst, r))], local_sem=s.loc1)
    src, dst = (T.r2q, T.aq) if codes else (T.r2s, T["as"])
    g.wait_ge(s.r2, count(p["high"]))
    g.remote_dma_fused([to(topo, [T.cores[c] for c in dsts], m, s["a%d" % r], view(src, 0), view(dst, r))],
                       local_sem=s.loc2)
    g.wait_ge(s.loc0, 2 * count(m))
    g.wait_ge(s.loc1, len(dsts) * count(m))
    g.wait_ge(s.loc2, count(m))


def rank_program(g, core, T, topo):
    r = T.rank_of(core)
    if r is None:
        for q in range(N):
            if topo.chip(T.cores[q]) == topo.chip(core) and core in plan(T, topo, q)["relays"]:
                relay_program(g, core, T, topo, q)
        return

    p = plan(T, topo, r)
    s = T.sem
    direct, cross = p["direct"], p["cross"]
    nd, nc = len(direct), len(cross)
    order = cross + direct + [r]
    v, te, sc, sy = g.vector, g.tensor, g.scalar, g.sync

    for i, c in enumerate(order):
        (sy if i % 2 == 0 else sc).dma_start(T.bt[:, cols(i, 1, 512)], T.b[:, cols(c, 1, 512)]).then_inc(s["ld%d" % i], 16)
    sc.dma_start(T.xt[:, :], T.x[:, :]).then_inc(s.ldx, 16)

    make_s(g, T, 0)

    for i in range(N):
        v.wait_ge(s["ld%d" % i], 16)
        v.quantize_mx(T.bq[:, cols(i)], T.bs[:, cols(i)], T.bt[:, cols(i, 1, 512)]).then_inc(s["q%d" % i], 1)
    v.wait_ge(s.ldx, 16)
    v.quantize_mx(T.xq[:], T.xs[:], T.xt[:]).then_inc(s.qxx, 1)

    def hop(n, sem, dst, src):
        rid, pid, _ = topo.addr(p["relays"][n])
        g.remote_dma(dst, src, sem, s.loc1, pid, rid, hop_mask(p, n))

    loc1 = sum(count(hop_mask(p, i % 2)) for i in range(nc)) + 2 * count(p["high"])
    for i in range(nc):
        g.wait_ge(s["q%d" % i], 1)
        n, k = i % 2, i // 2
        hop(n, s["r1%d" % k], T.r1q[:, cols(k)].bitcast(U8), T.bq[:, cols(i)].bitcast(U8))
        if i == 1:
            hop(2, s.r10, T.r1s[:, cols(0, 2)], T.bs[:, cols(0, 2)])
    hop(3, s.r10, T.r1s[:, cols(0, nc - 2)], T.bs[:, cols(2, nc - 2)])

    def send(i, src, dst):
        g.remote_dma_fused([to(topo, [T.cores[direct[i]]], p["low"], s["p%d" % r], src, dst)], local_sem=s.loc1)

    for i in range(nd):
        g.wait_ge(s["q%d" % (nc + i)], 1)
        send(i, T.bq[:, cols(nc + i)].bitcast(U8), T.gq[:, cols(r)].bitcast(U8))
        send(i, T.bs[:, cols(nc + i)], T.gs[:, cols(r)])
    loc1 += 2 * nd * count(p["low"])

    S = [(T.sq[:], T.ss[:])] + [(T.tq[:, cols(k)], T.ts[:, cols(k)]) for k in range(3)]
    te.wait_ge(s.sq, 1)
    for b in range(1, 4):
        te.wait_ge(s["s%d" % b], sum(2 * count(p["out"]) for x in PARTS if x[0] == b))
    sources = [r] + due(T, topo, r)

    def arrived(sem, mine, j):
        if j == r:
            te.wait_ge(mine, 1)
        else:
            q = plan(T, topo, j)
            te.wait_ge(s["%s%d" % (sem, j)], 2 * count(q["low"] if r in q["direct"] else q["out"]))

    for n, j in enumerate(sources):
        arrived("p", s["q%d" % (N - 1)], j)
        q, qs = (T.bq[:, cols(N - 1)], T.bs[:, cols(N - 1)]) if j == r else (T.gq[:, cols(j)], T.gs[:, cols(j)])
        for b in range(4):
            mm = te.matmul_mx(T.z[:, 512 * b:512 * b + 128], S[b][0], S[b][1], q, qs, n == 0, n == N - 1)
            if n == N - 1:
                mm.then_inc(s["z%d" % b], 1)

    for b in range(4):
        o, i = T.ht[:, b:512:4], T.z[:, 512 * b:512 * b + 128]
        if b % 2 == 0:
            sc.wait_ge(s["z%d" % b], 1)
            sc.activation(o, i, ActivationFunctionType.Relu, scale=C2).then_inc(s.hr, 1)
        else:
            v.wait_ge(s["z%d" % b], 1)
            v.tensor_scalar(o, i, 0.0, C2, AluOpType.max, AluOpType.mult).then_inc(s.hr, 1)
    v.wait_ge(s.hr, 4)
    v.quantize_mx(T.hq[:], T.hs[:], T.ht[:]).then_inc(s.hq, 1)

    g.wait_ge(s.hq, 1)
    sem = s["a%d" % r]
    ranks = [T.cores[c] for c in direct]
    for relays, src, mid, dst in ((p["far"], T.hq[:].bitcast(U8), T.r2q[:].bitcast(U8), T.aq[:, cols(r)].bitcast(U8)),
                                  (p["near"], T.hs[:], T.r2s[:], T["as"][:, cols(r)])):
        g.remote_dma_fused([to(topo, relays, p["high"], s.r2, src, mid), to(topo, ranks, p["low"], sem, src, dst)],
                           local_sem=s.loc2)
    loc2 = 2 * (count(p["high"]) + count(p["low"]))

    banks = [T.yp[:, 512 * i:512 * i + 128] for i in range(4)] + [T.z[:, 512 * i:512 * i + 128] for i in range(4)]
    te.wait_ge(s.qxx, 1)
    for n, j in enumerate(sources):
        arrived("a", s.hq, j)
        q, qs = (T.hq[:], T.hs[:]) if j == r else (T.aq[:, cols(j)], T["as"][:, cols(j)])
        te.matmul_mx(banks[n], q, qs, T.xq[:], T.xs[:], True, True).then_inc(s["ym%d" % j], 1)

    ns = [0, 0]
    for n, j in enumerate(sources):
        if n == 1:
            sy.wait_ge(s.hr, 4)
            sy.wait_ge(s["ym%d" % j], 1)
            sy.dma_start(T.h[:, :], T.ht[:]).then_inc(s.sth, 16)
        k = n % 2
        if k == 0:
            v.wait_ge(s["ym%d" % j], 1)
            v.tensor_copy(T.yt[:, cols(j)], banks[n]).then_inc(s["yc%d" % j], 1)
        else:
            sc.wait_ge(s["ym%d" % j], 1)
            sc.activation(T.yt[:, cols(j)], banks[n], ActivationFunctionType.Copy).then_inc(s["yc%d" % j], 1)
        e = (sy, sc)[k]
        e.wait_ge(s["yc%d" % j], 1)
        e.dma_start(T.y[:, cols(j)], T.yt[:, cols(j)]).then_inc((s.sty, s.sta)[k], 16)
        ns[k] += 16
    sc.wait_ge(s.sta, ns[1])
    sy.wait_ge(s.sty, ns[0])
    sy.wait_ge(s.sth, 16)
    g.wait_ge(s.loc1, loc1)
    g.wait_ge(s.loc2, loc2)
